import numpy as np
import ml_dtypes


def mxq(x, axis, fmt="e4m3"):
    dtype, down = {"e4m3": (ml_dtypes.float8_e4m3fn, 7), "e5m2": (ml_dtypes.float8_e5m2, 14)}[fmt]
    v = np.moveaxis(np.asarray(x, np.float32).astype(ml_dtypes.bfloat16).astype(np.float64), axis, -1)
    blocks = v.reshape(v.shape[:-1] + (-1, 32))
    amax = np.abs(blocks).max(-1, keepdims=True)
    byte = np.maximum(np.where(amax > 0, np.frexp(amax)[1] - 1 + 127, 0) - down, 1)
    scale = np.exp2(byte - 127.0)
    codes = (blocks / scale).astype(np.float32).astype(dtype).astype(np.float64)
    return np.moveaxis((codes * scale).reshape(v.shape), -1, axis)


WIDE = False


def mx_kscale(k):
    if not WIDE:
        return np.ones(k)
    levels = np.array([10, -10, 5, -5, 0])
    if k % 512:
        return np.exp2(np.random.permutation(np.resize(levels, k // 32))).repeat(32)
    a = np.empty((k // 512, 16))
    for p in range(k // 512):
        a[p, :8] = np.random.permutation(np.resize(levels, 8))
        for g in range(8):
            far = levels[np.abs(levels - a[p, g]) >= 10]
            a[p, g + 8] = far[np.random.randint(len(far))]
    return np.exp2(a.ravel()).repeat(32)


def f64(x):
    return np.asarray(x).astype(np.float64)


def striped(idx):
    return np.tile(idx.reshape(-1, 16).T, (8, 1)).astype(np.uint16)


def unstriped(offs):
    return offs[:16].T.reshape(-1).astype(np.int64)


E2M1 = np.array([0.0, 0.5, 1.0, 1.5, 2.0, 3.0, 4.0, 6.0, -0.0, -0.5, -1.0, -1.5, -2.0, -3.0, -4.0, -6.0])


def pack_weight(w, fmt):
    k, n = w.shape
    w = f64(np.asarray(w, np.float32).astype(ml_dtypes.bfloat16)).reshape(k // 32, 32, n)
    amax = np.abs(w).max(1)
    if fmt == "e4m3":
        byte = np.frexp(amax)[1] - 1 + 127 - 7
    else:
        mant, ex = np.frexp(amax / 6.0)
        byte = np.where(mant > 0.5, ex, ex - 1) + 127
    byte = np.clip(np.where(amax > 0, byte, 1), 1, 254)
    scaled = (w * np.exp2(127.0 - byte)[:, None, :]).reshape(k, n).astype(np.float32)
    by_word = np.ascontiguousarray(scaled.reshape(k // 512, 128, 4, n).transpose(0, 1, 3, 2))
    if fmt == "e4m3":
        words = by_word.astype(ml_dtypes.float8_e4m3fn).view(np.uint8)
    else:
        c = by_word.astype(ml_dtypes.float4_e2m1fn).view(np.uint8) & 0xF
        words = (c[..., 0::2] | (c[..., 1::2] << 4)).reshape(k // 512, 128, 2 * n)
    return np.ascontiguousarray(words), np.ascontiguousarray(byte.astype(np.uint8).reshape(k // 512, 16, n))


def unpack_weight(words, scales, fmt):
    g, _, n = scales.shape
    words = np.ascontiguousarray(words).reshape(g, 128, n, -1)
    if fmt == "e4m3":
        vals = words.view(ml_dtypes.float8_e4m3fn).astype(np.float64)
    else:
        nib = np.empty((g, 128, n, 4), np.uint8)
        nib[..., 0::2] = words & 0xF
        nib[..., 1::2] = words >> 4
        vals = E2M1[nib]
    vals = vals * np.repeat(np.exp2(scales.astype(np.float64) - 127.0), 8, axis=1)[..., None]
    return vals.transpose(0, 1, 3, 2).reshape(g * 512, n)


def relu2(v):
    return np.maximum(v, 0.0) ** 2


K, L, T, Q, E, C, D = 512, 1024, 1024, 1024, 2, 256, 256
H, N = 512, 128


def by_expert(wq, xq, C):
    return np.concatenate([wq[e].T @ xq[:, e * C:(e + 1) * C] for e in range(E)], axis=1)


def setup_inputs():
    n = np.random.standard_normal
    s = mx_kscale(K)
    v = mx_kscale(L)
    u = mx_kscale(H)
    slots1, slots2 = np.random.permutation(T)[:E * C], np.random.permutation(Q)[:E * D]
    x = pack_weight(n((K, T)) * s[:, None], "e4m3")
    z = pack_weight(n((L, Q)) * v[:, None], "e4m3")
    wz = [pack_weight(m, "e2m1") for m in n((E, L, H)) / np.sqrt(L) / v[None, :, None] * u]
    return {
        "x_words": x[0],
        "x_scales": x[1],
        "z_words": z[0],
        "z_scales": z[1],
        "w1": (n((E, K, H)) / np.sqrt(K) / s[None, :, None] * u).astype(np.float32),
        "wz_words": np.stack([m[0] for m in wz]),
        "wz_scales": np.stack([m[1] for m in wz]),
        "w2": (n((E, H, N)) / np.sqrt(H) / u[None, :, None] ** 2).astype(np.float32),
        "gate1": (np.tile(np.random.uniform(0.2, 1.0, E * C), (128, 1))).astype(np.float32),
        "gate2": (np.tile(np.random.uniform(0.2, 1.0, E * D), (128, 1))).astype(np.float32),
        "offs": striped(slots1),
        "offs2": striped(slots2),
    }


def reference(x_words, x_scales, z_words, z_scales, w1, wz_words, wz_scales, w2, gate1, gate2, offs, offs2):
    w1q = mxq(f64(w1), 1, "e4m3")
    wz = np.stack([unpack_weight(wz_words[e], wz_scales[e], "e2m1") for e in range(E)])
    w2q = mxq(f64(w2), 1, "e4m3")
    idx, idx2 = unstriped(offs), unstriped(offs2)
    xq = unpack_weight(x_words, x_scales, "e4m3")[:, idx]
    zq = unpack_weight(z_words, z_scales, "e4m3")[:, idx2]
    h = relu2(by_expert(w1q, xq, C))
    p = relu2(by_expert(wz, zq, D))
    out = np.zeros((N, T + Q))
    out[:, idx] = f64(gate1[:1]) * by_expert(w2q, mxq(h, 0, "e4m3"), C)
    out[:, T + idx2] = f64(gate2[:1]) * by_expert(w2q, mxq(p, 0, "e4m3"), D)
    return out

@@ -1,0 +1,235 @@
+from contextlib import ExitStack
+
+import concourse.mybir as mybir
+
+K, L, T, Q, E, C, H, N = 512, 1024, 1024, 1024, 2, 256, 512, 128
+P = 128
+FLOPS = 2 * E * C * (K * H + L * H + 2 * H * N)
+
+F32 = mybir.dt.float32
+BF16 = mybir.dt.bfloat16
+I32 = mybir.dt.int32
+U32 = mybir.dt.uint32
+U16 = mybir.dt.uint16
+U8 = mybir.dt.uint8
+FP8X4 = mybir.dt.float8_e4m3fn_x4
+FP4X4 = mybir.dt.float4_e2m1fn_x4
+ACT = mybir.ActivationFunctionType
+ALU = mybir.AluOpType
+
+
+def tile_moe_mmo_relu2_kernel(
+    tc, x_words, x_scales, z_words, z_scales, w1, wz_words, wz_scales, w2, gate1, gate2, offs, offs2, out
+):
+    nc = tc.nc
+    with ExitStack() as ctx:
+        keep = ctx.enter_context(tc.tile_pool(name="keep", bufs=1))
+        ring = ctx.enter_context(tc.tile_pool(name="ring", bufs=4))
+        ps1 = ctx.enter_context(tc.psum_pool(name="ps1", bufs=6))
+        ps2 = ctx.enter_context(tc.psum_pool(name="ps2", bufs=2))
+
+        def kt(name, shape, dt):
+            return keep.tile(shape, dt, name=name, align_bytes=64)
+
+        lists = [kt("list_text", [P, 32], U16), kt("list_patch", [P, 32], U16)]
+        xw = kt("xw", [P, T], I32)
+        xs = kt("xs", [P, T], U8)
+        zw = [kt("zw%d" % s, [P, Q], I32) for s in range(2)]
+        zs = kt("zs", [P, 2, Q], U8)
+        wzw_raw = kt("wzw_raw", [P, 4, 256], I32)
+        wzs_raw = kt("wzs_raw", [P, 4, H], U8)
+        wzw = [kt("wzw%d" % e, [P, 2, 2 * H], U8) for e in range(E)]
+        wzs = kt("wzs", [P, 4, H], U8)
+        w1_raw = [[kt("w1_raw%d%d" % (e, c), [P, 4, 256], F32) for c in range(2)] for e in range(E)]
+        w1_bf = [kt("w1_bf%d" % e, [P, H, 4], BF16) for e in range(E)]
+        w1_c = [kt("w1_c%d" % e, [P, H], U32) for e in range(E)]
+        w1_s = [kt("w1_s%d" % e, [P, H], U8) for e in range(E)]
+        w2_raw = kt("w2_raw", [P, E, 4, N], F32)
+        w2_bf = kt("w2_bf", [P, E, N, 4], BF16)
+        w2_c = kt("w2_c", [P, E * N], U32)
+        w2_s = kt("w2_s", [P, E * N], U8)
+        gates = [kt("gate%d" % m, [P, E * C], F32) for m in range(2)]
+        outs = [kt("out%d" % m, [P, T], F32) for m in range(2)]
+        xg = kt("xg", [P, E * C], U32)
+        xgs = kt("xgs", [P, E * C], U8)
+        zg = [kt("zg%d" % s, [P, E * C], U32) for s in range(2)]
+        zgs = [kt("zgs%d" % s, [P, E * C], U8) for s in range(2)]
+        warm = kt("warm", [P, 8], F32)
+
+        nc.vector.memset(xs[:].bitcast(I32), 0)
+        nc.vector.memset(zs[:].bitcast(I32), 0)
+        nc.vector.memset(wzs_raw[:].bitcast(I32), 0)
+        nc.vector.memset(warm[:], 0.0)
+        nc.scalar.activation(warm[:, 4:8], warm[:, 0:4], ACT.Square)
+        nc.vector.memset(outs[0][:], 0.0)
+        nc.vector.memset(outs[1][:], 0.0)
+
+        def load_w1(e, c):
+            nc.sync.dma_start(out=w1_raw[e][c][:], in_=w1[e].rearrange("(p j) c -> p j c", j=4)[:, :, 256 * c : 256 * c + 256])
+
+        def load_w2(e):
+            for j in range(4):
+                nc.sync.dma_start(
+                    out=w2_raw[:, e, j, :], in_=w2[e].rearrange("(b j u) n -> j b u n", j=4, u=8)[j]
+                )
+
+        load_w1(0, 0)
+        nc.sync.dma_start(lists[0][:], offs)
+        nc.sync.dma_start(out=xw[:], in_=x_words[0].rearrange("p t d -> p (t d)").bitcast(I32))
+        for q in range(4):
+            nc.sync.dma_start(out=xs[32 * q : 32 * q + 4, :].bitcast(I32), in_=x_scales[0, 4 * q : 4 * q + 4, :].bitcast(I32))
+        load_w1(0, 1)
+        load_w1(1, 0)
+        nc.sync.dma_start(lists[1][:], offs2)
+        nc.sync.dma_start(out=zw[0][:], in_=z_words[0].rearrange("p t d -> p (t d)").bitcast(I32))
+        for q in range(4):
+            nc.sync.dma_start(
+                out=zs[32 * q : 32 * q + 4].bitcast(I32),
+                in_=z_scales[:, 4 * q : 4 * q + 4, :].rearrange("s r n -> r s n").bitcast(I32),
+            )
+        load_w1(1, 1)
+        nc.sync.dma_start(out=zw[1][:], in_=z_words[1].rearrange("p t d -> p (t d)").bitcast(I32))
+        for q in range(4):
+            nc.gpsimd.dma_start(
+                out=wzs_raw[32 * q : 32 * q + 4].bitcast(I32),
+                in_=wz_scales[:, :, 4 * q : 4 * q + 4, :].rearrange("e s r n -> r (e s) n").bitcast(I32),
+            )
+        nc.sync.dma_start(out=wzw_raw[:], in_=wz_words.rearrange("e s p n -> p (e s) n").bitcast(I32))
+        load_w2(0)
+        nc.sync.dma_start(out=gates[0][:], in_=gate1)
+        load_w2(1)
+        nc.sync.dma_start(out=gates[1][:], in_=gate2)
+
+        def cast_w1(e, c):
+            nc.scalar.copy(
+                out=w1_bf[e][:].rearrange("p (t c b u) j -> p c t b u j", t=4, c=2, u=8)[:, c],
+                in_=w1_raw[e][c][:].rearrange("p j (b t u) -> p t b u j", t=4, u=8),
+            )
+
+        def quant_w1(e):
+            nc.vector.quantize_mx(out=w1_c[e][:].bitcast(FP8X4), scales=w1_s[e][:], in_=w1_bf[e][:].rearrange("p c j -> p (c j)"))
+
+        def cast_w2(e):
+            nc.scalar.copy(out=w2_bf[:, e], in_=w2_raw[:, e].rearrange("p j n -> p n j"))
+
+        def quant_w2(e):
+            nc.vector.quantize_mx(
+                out=w2_c[:, e * N : (e + 1) * N].bitcast(FP8X4),
+                scales=w2_s[:, e * N : (e + 1) * N],
+                in_=w2_bf[:, e].rearrange("p n j -> p (n j)"),
+            )
+
+        def gather(dst, window, m, lo, hi):
+            nc.vector.tensor_copy(dst[:, lo:hi], window.indirect(lists[m][:, lo // 16 : hi // 16]))
+
+        def gather_z(e):
+            for s in range(2):
+                gather(zg[s], zw[s][:].bitcast(U32), 1, e * C, (e + 1) * C)
+                gather(zgs[s], zs[:, s, :], 1, e * C, (e + 1) * C)
+
+        def permute_wz_scales():
+            nc.vector.tensor_copy(
+                out=wzs[:].bitcast(I32).rearrange("p g (t b w) -> p g t b w", t=4, w=2),
+                in_=wzs_raw[:].bitcast(I32).rearrange("p g (b t w) -> p g t b w", t=4, w=2),
+            )
+
+        def permute_wz(e):
+            nc.vector.tensor_copy(
+                out=wzw[e][:].bitcast(I32).rearrange("p s (t b w) -> p s t b w", t=4, w=4),
+                in_=wzw_raw[:, 2 * e : 2 * e + 2].rearrange("p s (b t w) -> p s t b w", t=4, w=4),
+            )
+
+        hid = {}
+
+        def first_layer(m, e):
+            act = ring.tile([P, C * 4], BF16, name="act", align_bytes=64)
+            for half in range(2):
+                lo = e * C + half * 128
+                bank = ps1.tile([P, 4, 128], F32, name="bank")
+                for t in range(4):
+                    if m == 0:
+                        nc.tensor.matmul_mx(
+                            out=bank[:, t, :],
+                            lhsT=w1_c[e][:, 128 * t : 128 * t + 128].bitcast(FP8X4),
+                            lhsT_scale=w1_s[e][:, 128 * t : 128 * t + 128],
+                            rhs=xg[:, lo : lo + 128].bitcast(FP8X4),
+                            rhs_scale=xgs[:, lo : lo + 128],
+                            start=True,
+                            stop=True,
+                        )
+                    else:
+                        for s in range(2):
+                            nc.tensor.matmul_mx(
+                                out=bank[:, t, :],
+                                lhsT=wzw[e][:, s, 256 * t : 256 * t + 256].bitcast(FP4X4),
+                                lhsT_scale=wzs[:, 2 * e + s, 128 * t : 128 * t + 128],
+                                rhs=zg[s][:, lo : lo + 128].bitcast(FP8X4),
+                                rhs_scale=zgs[s][:, lo : lo + 128],
+                                start=(s == 0),
+                                stop=(s == 1),
+                            )
+                pos = ring.tile([P, 128, 4], F32, name="pos", align_bytes=64)
+                nc.scalar.activation(pos[:], bank[:].rearrange("p t n -> p n t"), ACT.Relu)
+                nc.scalar.activation(
+                    act[:, 512 * half : 512 * half + 512], pos[:].rearrange("p n t -> p (n t)"), ACT.Square
+                )
+            hid[m, e] = act
+
+        res = {}
+
+        def second_layer(m, e):
+            hc = ring.tile([P, C], U32, name="hc", align_bytes=64)
+            hs = ring.tile([P, C], U8, name="hs", align_bytes=64)
+            nc.vector.quantize_mx(out=hc[:].bitcast(FP8X4), scales=hs[:], in_=hid[m, e][:])
+            acc = ps2.tile([P, C], F32, name="acc")
+            nc.tensor.matmul_mx(
+                out=acc[:],
+                lhsT=w2_c[:, e * N : (e + 1) * N].bitcast(FP8X4),
+                lhsT_scale=w2_s[:, e * N : (e + 1) * N],
+                rhs=hc[:].bitcast(FP8X4),
+                rhs_scale=hs[:],
+                start=True,
+                stop=True,
+            )
+            res[m, e] = acc
+
+        def scatter(m, e):
+            gated = ring.tile([P, C], F32, name="gated", align_bytes=64)
+            nc.vector.tensor_tensor(gated[:], res[m, e][:], gates[m][:, e * C : (e + 1) * C], ALU.mult)
+            nc.vector.tensor_copy(outs[m][:].indirect(lists[m][:, 16 * e : 16 * e + 16]), gated[:])
+
+        cast_w1(0, 0)
+        gather(xg, xw[:].bitcast(U32), 0, 0, 2 * C)
+        gather(xgs, xs[:], 0, 0, 2 * C)
+        cast_w1(0, 1)
+        quant_w1(0)
+        cast_w1(1, 0)
+        first_layer(0, 0)
+        gather(zg[0], zw[0][:].bitcast(U32), 1, 0, 2 * C)
+        gather(zgs[0], zs[:, 0, :], 1, 0, 2 * C)
+        cast_w1(1, 1)
+        quant_w1(1)
+        cast_w2(0)
+        first_layer(0, 1)
+        gather(zg[1], zw[1][:].bitcast(U32), 1, 0, C)
+        gather(zgs[1], zs[:, 1, :], 1, 0, C)
+        permute_wz_scales()
+        permute_wz(0)
+        cast_w2(1)
+        first_layer(1, 0)
+        quant_w2(0)
+        second_layer(0, 0)
+        gather(zg[1], zw[1][:].bitcast(U32), 1, C, 2 * C)
+        gather(zgs[1], zs[:, 1, :], 1, C, 2 * C)
+        permute_wz(1)
+        first_layer(1, 1)
+        scatter(0, 0)
+        quant_w2(1)
+        second_layer(0, 1)
+        second_layer(1, 0)
+        scatter(0, 1)
+        nc.sync.dma_start(out=out[:, 0:T], in_=outs[0][:])
+        scatter(1, 0)
+        second_layer(1, 1)
+        scatter(1, 1)
+        nc.sync.dma_start(out=out[:, T : T + Q], in_=outs[1][:])

@@ -16,6 +16,9 @@ FP8X4 = mybir.dt.float8_e4m3fn_x4
 FP4X4 = mybir.dt.float4_e2m1fn_x4
 ACT = mybir.ActivationFunctionType
 ALU = mybir.AluOpType
+FUSED = True
+HALF = [[1,1]]
+C1G = []
 
 
 def tile_moe_mmo_relu2_kernel(
@@ -24,136 +27,144 @@ def tile_moe_mmo_relu2_kernel(
     nc = tc.nc
     with ExitStack() as ctx:
         keep = ctx.enter_context(tc.tile_pool(name="keep", bufs=1))
-        ring = ctx.enter_context(tc.tile_pool(name="ring", bufs=4))
-        ps1 = ctx.enter_context(tc.psum_pool(name="ps1", bufs=6))
-        ps2 = ctx.enter_context(tc.psum_pool(name="ps2", bufs=2))
+        vout = ctx.enter_context(tc.tile_pool(name="vout", bufs=24))
+        sout = ctx.enter_context(tc.tile_pool(name="sout", bufs=16))
+        psum = ctx.enter_context(tc.psum_pool(name="psum", bufs=8))
+
+        def vt(name, shape, dt):
+            return vout.tile(shape, dt, name=name, tag="v", align_bytes=64)
+
+        def sct(name, shape, dt):
+            return sout.tile(shape, dt, name=name, tag="s", align_bytes=64)
 
         def kt(name, shape, dt):
             return keep.tile(shape, dt, name=name, align_bytes=64)
 
-        lists = [kt("list_text", [P, 32], U16), kt("list_patch", [P, 32], U16)]
+        lists = [kt("liscttext", [P, 32], U16), kt("lisctpatch", [P, 32], U16)]
         xw = kt("xw", [P, T], I32)
         xs = kt("xs", [P, T], U8)
         zw = [kt("zw%d" % s, [P, Q], I32) for s in range(2)]
         zs = kt("zs", [P, 2, Q], U8)
         wzw_raw = kt("wzw_raw", [P, 4, 256], I32)
         wzs_raw = kt("wzs_raw", [P, 4, H], U8)
-        wzw = [kt("wzw%d" % e, [P, 2, 2 * H], U8) for e in range(E)]
-        wzs = kt("wzs", [P, 4, H], U8)
         w1_raw = [[kt("w1_raw%d%d" % (e, c), [P, 4, 256], F32) for c in range(2)] for e in range(E)]
-        w1_bf = [kt("w1_bf%d" % e, [P, H, 4], BF16) for e in range(E)]
-        w1_c = [kt("w1_c%d" % e, [P, H], U32) for e in range(E)]
         w1_s = [kt("w1_s%d" % e, [P, H], U8) for e in range(E)]
         w2_raw = kt("w2_raw", [P, E, 4, N], F32)
-        w2_bf = kt("w2_bf", [P, E, N, 4], BF16)
-        w2_c = kt("w2_c", [P, E * N], U32)
-        w2_s = kt("w2_s", [P, E * N], U8)
         gates = [kt("gate%d" % m, [P, E * C], F32) for m in range(2)]
         outs = [kt("out%d" % m, [P, T], F32) for m in range(2)]
-        xg = kt("xg", [P, E * C], U32)
-        xgs = kt("xgs", [P, E * C], U8)
-        zg = [kt("zg%d" % s, [P, E * C], U32) for s in range(2)]
-        zgs = [kt("zgs%d" % s, [P, E * C], U8) for s in range(2)]
-        warm = kt("warm", [P, 8], F32)
 
+        w2_s = [kt("w2_s%d" % e, [P, N], U8) for e in range(E)]
+        tl = {}
         nc.vector.memset(xs[:].bitcast(I32), 0)
         nc.vector.memset(zs[:].bitcast(I32), 0)
         nc.vector.memset(wzs_raw[:].bitcast(I32), 0)
-        nc.vector.memset(warm[:], 0.0)
-        nc.scalar.activation(warm[:, 4:8], warm[:, 0:4], ACT.Square)
-        nc.vector.memset(outs[0][:], 0.0)
-        nc.vector.memset(outs[1][:], 0.0)
+        nc.gpsimd.memset(outs[0][:], 0.0)
+        nc.gpsimd.memset(outs[1][:], 0.0)
 
-        def load_w1(e, c):
-            nc.sync.dma_start(out=w1_raw[e][c][:], in_=w1[e].rearrange("(p j) c -> p j c", j=4)[:, :, 256 * c : 256 * c + 256])
-
-        def load_w2(e):
-            for j in range(4):
+        def load(name):
+            q = int(name[2]) if name[:2] in ("xs", "zs", "ws") else 0
+            rows = slice(32 * q, 32 * q + 4)
+            src = slice(4 * q, 4 * q + 4)
+            if name == "offs":
+                nc.sync.dma_start(lists[0][:], offs)
+            elif name == "offs2":
+                nc.sync.dma_start(lists[1][:], offs2)
+            elif name == "xw":
+                nc.sync.dma_start(out=xw[:], in_=x_words[0].rearrange("p t d -> p (t d)").bitcast(I32))
+            elif name[:2] == "zw":
+                s = int(name[2])
+                nc.sync.dma_start(out=zw[s][:], in_=z_words[s].rearrange("p t d -> p (t d)").bitcast(I32))
+            elif name[:2] == "xs":
+                nc.sync.dma_start(out=xs[rows, :].bitcast(I32), in_=x_scales[0, src, :].bitcast(I32))
+            elif name[:2] == "zs":
+                nc.sync.dma_start(out=zs[rows].bitcast(I32), in_=z_scales[:, src, :].rearrange("s r n -> r s n").bitcast(I32))
+            elif name[:2] == "ws":
                 nc.sync.dma_start(
-                    out=w2_raw[:, e, j, :], in_=w2[e].rearrange("(b j u) n -> j b u n", j=4, u=8)[j]
+                    out=wzs_raw[rows].bitcast(I32), in_=wz_scales[:, :, src, :].rearrange("e s r n -> r (e s) n").bitcast(I32)
                 )
+            elif name == "wz":
+                nc.sync.dma_start(out=wzw_raw[:], in_=wz_words.rearrange("e s p n -> p (e s) n").bitcast(I32))
+            elif name[:2] == "w1":
+                i = ["a", "b", "c", "d"].index(name[2])
+                e, c = i // 2, i % 2
+                nc.sync.dma_start(out=w1_raw[e][c][:], in_=w1[e].rearrange("(p j) c -> p j c", j=4)[:, :, 256 * c : 256 * c + 256])
+            elif name[:2] == "w2":
+                e, j = int(name[2]), int(name[3])
+                nc.sync.dma_start(out=w2_raw[:, e, j, :], in_=w2[e].rearrange("(b j u) n -> j b u n", j=4, u=8)[j])
+            else:
+                m = int(name[1])
+                nc.sync.dma_start(out=gates[m][:], in_=(gate1, gate2)[m])
 
-        load_w1(0, 0)
-        nc.sync.dma_start(lists[0][:], offs)
-        nc.sync.dma_start(out=xw[:], in_=x_words[0].rearrange("p t d -> p (t d)").bitcast(I32))
-        for q in range(4):
-            nc.sync.dma_start(out=xs[32 * q : 32 * q + 4, :].bitcast(I32), in_=x_scales[0, 4 * q : 4 * q + 4, :].bitcast(I32))
-        load_w1(0, 1)
-        load_w1(1, 0)
-        nc.sync.dma_start(lists[1][:], offs2)
-        nc.sync.dma_start(out=zw[0][:], in_=z_words[0].rearrange("p t d -> p (t d)").bitcast(I32))
-        for q in range(4):
-            nc.sync.dma_start(
-                out=zs[32 * q : 32 * q + 4].bitcast(I32),
-                in_=z_scales[:, 4 * q : 4 * q + 4, :].rearrange("s r n -> r s n").bitcast(I32),
-            )
-        load_w1(1, 1)
-        nc.sync.dma_start(out=zw[1][:], in_=z_words[1].rearrange("p t d -> p (t d)").bitcast(I32))
-        for q in range(4):
-            nc.gpsimd.dma_start(
-                out=wzs_raw[32 * q : 32 * q + 4].bitcast(I32),
-                in_=wz_scales[:, :, 4 * q : 4 * q + 4, :].rearrange("e s r n -> r (e s) n").bitcast(I32),
-            )
-        nc.sync.dma_start(out=wzw_raw[:], in_=wz_words.rearrange("e s p n -> p (e s) n").bitcast(I32))
-        load_w2(0)
-        nc.sync.dma_start(out=gates[0][:], in_=gate1)
-        load_w2(1)
-        nc.sync.dma_start(out=gates[1][:], in_=gate2)
+        for name in ["xs3","w1c","offs2","xw","xs1","xs2","offs","w1d","zs3","xs0","w1a","zs1","zs2","zs0","w1b","ws0","ws2","ws3","wz","ws1","zw1","w212","zw0","w203","w201","w210","w200","w202","w213","w211","g0","g1"]:
+            load(name)
 
         def cast_w1(e, c):
-            nc.scalar.copy(
-                out=w1_bf[e][:].rearrange("p (t c b u) j -> p c t b u j", t=4, c=2, u=8)[:, c],
+            if c == 0:
+                tl["w1_bf", e] = (kt if [e, c] in C1G else sct)("w1_bf%d" % e, [P, H, 4], BF16)
+            (nc.gpsimd.tensor_copy if [e, c] in C1G else nc.scalar.copy)(
+                out=tl["w1_bf", e][:].rearrange("p (t c b u) j -> p c t b u j", t=4, c=2, u=8)[:, c],
                 in_=w1_raw[e][c][:].rearrange("p j (b t u) -> p t b u j", t=4, u=8),
             )
 
         def quant_w1(e):
-            nc.vector.quantize_mx(out=w1_c[e][:].bitcast(FP8X4), scales=w1_s[e][:], in_=w1_bf[e][:].rearrange("p c j -> p (c j)"))
-
-        def cast_w2(e):
-            nc.scalar.copy(out=w2_bf[:, e], in_=w2_raw[:, e].rearrange("p j n -> p n j"))
-
-        def quant_w2(e):
+            tl["w1_c", e] = vt("w1_c%d" % e, [P, H], U32)
             nc.vector.quantize_mx(
-                out=w2_c[:, e * N : (e + 1) * N].bitcast(FP8X4),
-                scales=w2_s[:, e * N : (e + 1) * N],
-                in_=w2_bf[:, e].rearrange("p n j -> p (n j)"),
+                out=tl["w1_c", e][:].bitcast(FP8X4), scales=w1_s[e][:], in_=tl["w1_bf", e][:].rearrange("p c j -> p (c j)")
             )
 
-        def gather(dst, window, m, lo, hi):
-            nc.vector.tensor_copy(dst[:, lo:hi], window.indirect(lists[m][:, lo // 16 : hi // 16]))
+        def cast_w2(e):
+            tl["w2_bf", e] = kt("w2_bf%d" % e, [P, N, 4], BF16)
+            nc.gpsimd.tensor_copy(out=tl["w2_bf", e][:], in_=w2_raw[:, e].rearrange("p j n -> p n j"))
 
-        def gather_z(e):
-            for s in range(2):
-                gather(zg[s], zw[s][:].bitcast(U32), 1, e * C, (e + 1) * C)
-                gather(zgs[s], zs[:, s, :], 1, e * C, (e + 1) * C)
+        def quant_w2(e):
+            tl["w2_c", e] = vt("w2_c%d" % e, [P, N], U32)
+            nc.vector.quantize_mx(
+                out=tl["w2_c", e][:].bitcast(FP8X4), scales=w2_s[e][:], in_=tl["w2_bf", e][:].rearrange("p n j -> p (n j)")
+            )
+
+        windows = {
+            "xw": (U32, xw[:].bitcast(U32), 0),
+            "xs": (U8, xs[:], 0),
+            "zw0": (U32, zw[0][:].bitcast(U32), 1),
+            "zw1": (U32, zw[1][:].bitcast(U32), 1),
+            "zs0": (U8, zs[:, 0, :], 1),
+            "zs1": (U8, zs[:, 1, :], 1),
+        }
+
+        def gather(what, e0, e1):
+            dt, window, m = windows[what]
+            dst = vt("g_%s%d" % (what, e0), [P, (e1 - e0) * C], dt)
+            nc.vector.tensor_copy(dst[:], window.indirect(lists[m][:, 16 * e0 : 16 * e1]))
+            for e in range(e0, e1):
+                tl[what, e] = dst[:, (e - e0) * C : (e - e0 + 1) * C]
 
         def permute_wz_scales():
+            tl["wzs"] = vt("wzs", [P, 4, H], U8)
             nc.vector.tensor_copy(
-                out=wzs[:].bitcast(I32).rearrange("p g (t b w) -> p g t b w", t=4, w=2),
+                out=tl["wzs"][:].bitcast(I32).rearrange("p g (t b w) -> p g t b w", t=4, w=2),
                 in_=wzs_raw[:].bitcast(I32).rearrange("p g (b t w) -> p g t b w", t=4, w=2),
             )
 
         def permute_wz(e):
+            tl["wzw", e] = vt("wzw%d" % e, [P, 2, 2 * H], U8)
             nc.vector.tensor_copy(
-                out=wzw[e][:].bitcast(I32).rearrange("p s (t b w) -> p s t b w", t=4, w=4),
+                out=tl["wzw", e][:].bitcast(I32).rearrange("p s (t b w) -> p s t b w", t=4, w=4),
                 in_=wzw_raw[:, 2 * e : 2 * e + 2].rearrange("p s (b t w) -> p s t b w", t=4, w=4),
             )
 
-        hid = {}
-
         def first_layer(m, e):
-            act = ring.tile([P, C * 4], BF16, name="act", align_bytes=64)
+            pos = sct("pos%d%d" % (m, e), [P, 2, 128, 4], F32)
             for half in range(2):
-                lo = e * C + half * 128
-                bank = ps1.tile([P, 4, 128], F32, name="bank")
+                cols = slice(half * 128, half * 128 + 128)
+                bank = psum.tile([P, 4, 128], F32, name="bank", tag="bank")
                 for t in range(4):
                     if m == 0:
                         nc.tensor.matmul_mx(
                             out=bank[:, t, :],
-                            lhsT=w1_c[e][:, 128 * t : 128 * t + 128].bitcast(FP8X4),
+                            lhsT=tl["w1_c", e][:, 128 * t : 128 * t + 128].bitcast(FP8X4),
                             lhsT_scale=w1_s[e][:, 128 * t : 128 * t + 128],
-                            rhs=xg[:, lo : lo + 128].bitcast(FP8X4),
-                            rhs_scale=xgs[:, lo : lo + 128],
+                            rhs=tl["xw", e][:, cols].bitcast(FP8X4),
+                            rhs_scale=tl["xs", e][:, cols],
                             start=True,
                             stop=True,
                         )
@@ -161,75 +172,69 @@ def tile_moe_mmo_relu2_kernel(
                         for s in range(2):
                             nc.tensor.matmul_mx(
                                 out=bank[:, t, :],
-                                lhsT=wzw[e][:, s, 256 * t : 256 * t + 256].bitcast(FP4X4),
-                                lhsT_scale=wzs[:, 2 * e + s, 128 * t : 128 * t + 128],
-                                rhs=zg[s][:, lo : lo + 128].bitcast(FP8X4),
-                                rhs_scale=zgs[s][:, lo : lo + 128],
+                                lhsT=tl["wzw", e][:, s, 256 * t : 256 * t + 256].bitcast(FP4X4),
+                                lhsT_scale=tl["wzs"][:, 2 * e + s, 128 * t : 128 * t + 128],
+                                rhs=tl["zw%d" % s, e][:, cols].bitcast(FP8X4),
+                                rhs_scale=tl["zs%d" % s, e][:, cols],
                                 start=(s == 0),
                                 stop=(s == 1),
                             )
-                pos = ring.tile([P, 128, 4], F32, name="pos", align_bytes=64)
-                nc.scalar.activation(pos[:], bank[:].rearrange("p t n -> p n t"), ACT.Relu)
-                nc.scalar.activation(
-                    act[:, 512 * half : 512 * half + 512], pos[:].rearrange("p n t -> p (n t)"), ACT.Square
-                )
-            hid[m, e] = act
+                nc.scalar.activation(pos[:, half], bank[:].rearrange("p t n -> p n t"), ACT.Relu)
+            tl["pos", m, e] = pos
 
-        res = {}
+        def pieces(m, e):
+            return ((0, 128), (128, 256)) if [m, e] in HALF else ((0, 256),)
+
+        def square(m, e):
+            act = sct("act%d%d" % (m, e), [P, C * 4], BF16)
+            flat = tl["pos", m, e][:].rearrange("p h n t -> p (h n t)")
+            for lo, hi in pieces(m, e):
+                nc.scalar.activation(act[:, 4 * lo : 4 * hi], flat[:, 4 * lo : 4 * hi], ACT.Square)
+            tl["act", m, e] = act
 
         def second_layer(m, e):
-            hc = ring.tile([P, C], U32, name="hc", align_bytes=64)
-            hs = ring.tile([P, C], U8, name="hs", align_bytes=64)
-            nc.vector.quantize_mx(out=hc[:].bitcast(FP8X4), scales=hs[:], in_=hid[m, e][:])
-            acc = ps2.tile([P, C], F32, name="acc")
-            nc.tensor.matmul_mx(
-                out=acc[:],
-                lhsT=w2_c[:, e * N : (e + 1) * N].bitcast(FP8X4),
-                lhsT_scale=w2_s[:, e * N : (e + 1) * N],
-                rhs=hc[:].bitcast(FP8X4),
-                rhs_scale=hs[:],
-                start=True,
-                stop=True,
-            )
-            res[m, e] = acc
+            hc = vt("hc%d%d" % (m, e), [P, C], U32)
+            hs = kt("hs%d%d" % (m, e), [P, C], U8)
+            for lo, hi in pieces(m, e):
+                nc.vector.quantize_mx(out=hc[:, lo:hi].bitcast(FP8X4), scales=hs[:, lo:hi], in_=tl["act", m, e][:, 4 * lo : 4 * hi])
+                acc = psum.tile([P, hi - lo], F32, name="acc", tag="bank")
+                nc.tensor.matmul_mx(
+                    out=acc[:],
+                    lhsT=tl["w2_c", e][:].bitcast(FP8X4),
+                    lhsT_scale=w2_s[e][:],
+                    rhs=hc[:, lo:hi].bitcast(FP8X4),
+                    rhs_scale=hs[:, lo:hi],
+                    start=True,
+                    stop=True,
+                )
+                tl["acc", m, e, lo] = acc
+
+        def evacuate(m, e):
+            ev = sct("ev%d%d" % (m, e), [P, C], F32)
+            for lo, hi in pieces(m, e):
+                if FUSED:
+                    nc.scalar.copy(ev[:, lo:hi], tl["acc", m, e, lo][:])
+                else:
+                    nc.vector.tensor_tensor(ev[:, lo:hi], tl["acc", m, e, lo][:], gates[m][:, e * C + lo : e * C + hi], ALU.mult)
+            tl["ev", m, e] = ev
 
         def scatter(m, e):
-            gated = ring.tile([P, C], F32, name="gated", align_bytes=64)
-            nc.vector.tensor_tensor(gated[:], res[m, e][:], gates[m][:, e * C : (e + 1) * C], ALU.mult)
-            nc.vector.tensor_copy(outs[m][:].indirect(lists[m][:, 16 * e : 16 * e + 16]), gated[:])
+            for lo, hi in pieces(m, e):
+                window = outs[m][:].indirect(lists[m][:, (e * C + lo) // 16 : (e * C + hi) // 16])
+                if FUSED:
+                    nc.vector.tensor_tensor(window, tl["ev", m, e][:, lo:hi], gates[m][:, e * C + lo : e * C + hi], ALU.mult)
+                else:
+                    nc.vector.tensor_copy(window, tl["ev", m, e][:, lo:hi])
 
-        cast_w1(0, 0)
-        gather(xg, xw[:].bitcast(U32), 0, 0, 2 * C)
-        gather(xgs, xs[:], 0, 0, 2 * C)
-        cast_w1(0, 1)
-        quant_w1(0)
-        cast_w1(1, 0)
-        first_layer(0, 0)
-        gather(zg[0], zw[0][:].bitcast(U32), 1, 0, 2 * C)
-        gather(zgs[0], zs[:, 0, :], 1, 0, 2 * C)
-        cast_w1(1, 1)
-        quant_w1(1)
-        cast_w2(0)
-        first_layer(0, 1)
-        gather(zg[1], zw[1][:].bitcast(U32), 1, 0, C)
-        gather(zgs[1], zs[:, 1, :], 1, 0, C)
-        permute_wz_scales()
-        permute_wz(0)
-        cast_w2(1)
-        first_layer(1, 0)
-        quant_w2(0)
-        second_layer(0, 0)
-        gather(zg[1], zw[1][:].bitcast(U32), 1, C, 2 * C)
-        gather(zgs[1], zs[:, 1, :], 1, C, 2 * C)
-        permute_wz(1)
-        first_layer(1, 1)
-        scatter(0, 0)
-        quant_w2(1)
-        second_layer(0, 1)
-        second_layer(1, 0)
-        scatter(0, 1)
-        nc.sync.dma_start(out=out[:, 0:T], in_=outs[0][:])
-        scatter(1, 0)
-        second_layer(1, 1)
-        scatter(1, 1)
-        nc.sync.dma_start(out=out[:, T : T + Q], in_=outs[1][:])
+        def store(m):
+            nc.sync.dma_start(out=out[:, m * T : (m + 1) * T], in_=outs[m][:])
+
+        table = {
+            "g": gather, "q1": quant_w1, "c2": cast_w2, "q2": quant_w2, "ps": permute_wz_scales, "pw": permute_wz,
+            "f": first_layer, "sq": square, "s": second_layer, "ev": evacuate, "x": scatter, "o": store,
+        }
+        for step in [["c2",0],["c1",1,"c"],["c1",1,"d"],["g","xw",0,2],["g","xs",0,2],["c1",0,"a"],["g","zs0",0,2],["q1",1],["g","zs1",0,2],["c1",0,"b"],["q1",0],["pw",0],["g","zw1",0,2],["f",0,1],["g","zw0",0,1],["ps"],["sq",0,1],["g","zw0",1,2],["f",0,0],["c2",1],["q2",0],["sq",0,0],["pw",1],["f",1,0],["s",0,0],["ev",0,0],["q2",1],["s",0,1],["sq",1,0],["ev",0,1],["f",1,1],["sq",1,1],["s",1,0],["x",0,0],["x",0,1],["ev",1,0],["o",0],["s",1,1],["x",1,0],["ev",1,1],["x",1,1],["o",1]]:
+            if step[0] == "c1":
+                cast_w1(step[1], ["a", "b", "c", "d"].index(step[2]) % 2)
+            else:
+                table[step[0]](*step[1:])

@@ -47,7 +47,7 @@ def tile_moe_mmo_relu2_kernel(
         zs = kt("zs", [P, 2, Q], U8)
         wzw_raw = kt("wzw_raw", [P, 4, 256], I32)
         wzs_raw = kt("wzs_raw", [P, 4, H], U8)
-        w1_raw = [[kt("w1_raw%d%d" % (e, c), [P, 4, 256], F32) for c in range(2)] for e in range(E)]
+        w1_raw = [kt("w1_raw%d" % e, [P, 4, H], F32) for e in range(E)]
         w1_s = [kt("w1_s%d" % e, [P, H], U8) for e in range(E)]
         w2_raw = kt("w2_raw", [P, E, 4, N], F32)
         gates = [kt("gate%d" % m, [P, E * C], F32) for m in range(2)]
@@ -58,13 +58,12 @@ def tile_moe_mmo_relu2_kernel(
         nc.vector.memset(xs[:].bitcast(I32), 0)
         nc.vector.memset(zs[:].bitcast(I32), 0)
         nc.vector.memset(wzs_raw[:].bitcast(I32), 0)
-        nc.gpsimd.memset(outs[0][:], 0.0)
-        nc.gpsimd.memset(outs[1][:], 0.0)
+        nc.vector.memset(outs[0][:], 0.0)
+        nc.vector.memset(outs[1][:], 0.0)
 
         def load(name):
             q = int(name[2]) if name[:2] in ("xs", "zs", "ws") else 0
-            rows = slice(32 * q, 32 * q + 4)
-            src = slice(4 * q, 4 * q + 4)
+            rows = slice(q, P, 32)
             if name == "offs":
                 nc.sync.dma_start(lists[0][:], offs)
             elif name == "offs2":
@@ -75,19 +74,18 @@ def tile_moe_mmo_relu2_kernel(
                 s = int(name[2])
                 nc.sync.dma_start(out=zw[s][:], in_=z_words[s].rearrange("p t d -> p (t d)").bitcast(I32))
             elif name[:2] == "xs":
-                nc.sync.dma_start(out=xs[rows, :].bitcast(I32), in_=x_scales[0, src, :].bitcast(I32))
+                nc.sync.dma_start(out=xs[rows, :].bitcast(I32), in_=x_scales[0].rearrange("(g r) n -> r g n", r=4)[q].bitcast(I32))
             elif name[:2] == "zs":
-                nc.sync.dma_start(out=zs[rows].bitcast(I32), in_=z_scales[:, src, :].rearrange("s r n -> r s n").bitcast(I32))
+                nc.sync.dma_start(out=zs[rows].bitcast(I32), in_=z_scales.rearrange("s (g r) n -> r g s n", r=4)[q].bitcast(I32))
             elif name[:2] == "ws":
                 nc.sync.dma_start(
-                    out=wzs_raw[rows].bitcast(I32), in_=wz_scales[:, :, src, :].rearrange("e s r n -> r (e s) n").bitcast(I32)
+                    out=wzs_raw[rows].bitcast(I32), in_=wz_scales.rearrange("e s (g r) n -> r g (e s) n", r=4)[q].bitcast(I32)
                 )
             elif name == "wz":
                 nc.sync.dma_start(out=wzw_raw[:], in_=wz_words.rearrange("e s p n -> p (e s) n").bitcast(I32))
             elif name[:2] == "w1":
-                i = ["a", "b", "c", "d"].index(name[2])
-                e, c = i // 2, i % 2
-                nc.sync.dma_start(out=w1_raw[e][c][:], in_=w1[e].rearrange("(p j) c -> p j c", j=4)[:, :, 256 * c : 256 * c + 256])
+                e = ["A", "B"].index(name[2])
+                nc.sync.dma_start(out=w1_raw[e][:], in_=w1[e].rearrange("(p j) c -> p j c", j=4))
             elif name[:2] == "w2":
                 e, j = int(name[2]), int(name[3])
                 nc.sync.dma_start(out=w2_raw[:, e, j, :], in_=w2[e].rearrange("(b j u) n -> j b u n", j=4, u=8)[j])
@@ -95,16 +93,17 @@ def tile_moe_mmo_relu2_kernel(
                 m = int(name[1])
                 nc.sync.dma_start(out=gates[m][:], in_=(gate1, gate2)[m])
 
-        for name in ["xs3","w1c","offs2","xw","xs1","xs2","offs","w1d","zs3","xs0","w1a","zs1","zs2","zs0","w1b","ws0","ws2","ws3","wz","ws1","zw1","w212","zw0","w203","w201","w210","w200","w202","w213","w211","g0","g1"]:
+        for name in ["w1A","xs0","xs1","xs3","xs2","xw","offs","w1B","zs2","zs1","offs2","zs3","zs0","zw1","ws2","ws3","ws1","ws0","zw0","w212","w211","w203","wz","w201","w213","w200","w210","w202","g1","g0"]:
             load(name)
 
         def cast_w1(e, c):
             if c == 0:
                 tl["w1_bf", e] = (kt if [e, c] in C1G else sct)("w1_bf%d" % e, [P, H, 4], BF16)
-            (nc.gpsimd.tensor_copy if [e, c] in C1G else nc.scalar.copy)(
-                out=tl["w1_bf", e][:].rearrange("p (t c b u) j -> p c t b u j", t=4, c=2, u=8)[:, c],
-                in_=w1_raw[e][c][:].rearrange("p j (b t u) -> p t b u j", t=4, u=8),
-            )
+            for t in (2 * c, 2 * c + 1):
+                nc.scalar.copy(
+                    out=tl["w1_bf", e][:].rearrange("p (t b h l) j -> p t b h j l", t=4, h=2, l=4)[:, t],
+                    in_=w1_raw[e][:].rearrange("p j (b t h l) -> p t b h j l", t=4, h=2, l=4)[:, t],
+                )
 
         def quant_w1(e):
             tl["w1_c", e] = vt("w1_c%d" % e, [P, H], U32)
@@ -113,8 +112,10 @@ def tile_moe_mmo_relu2_kernel(
             )
 
         def cast_w2(e):
-            tl["w2_bf", e] = kt("w2_bf%d" % e, [P, N, 4], BF16)
-            nc.gpsimd.tensor_copy(out=tl["w2_bf", e][:], in_=w2_raw[:, e].rearrange("p j n -> p n j"))
+            tl["w2_bf", e] = vt("w2_bf%d" % e, [P, N, 4], BF16)
+            nc.vector.tensor_copy(
+                out=tl["w2_bf", e][:].rearrange("p (a l) j -> p a j l", l=4), in_=w2_raw[:, e].rearrange("p j (a l) -> p a j l", l=4)
+            )
 
         def quant_w2(e):
             tl["w2_c", e] = vt("w2_c%d" % e, [P, N], U32)
@@ -233,7 +234,7 @@ def tile_moe_mmo_relu2_kernel(
             "g": gather, "q1": quant_w1, "c2": cast_w2, "q2": quant_w2, "ps": permute_wz_scales, "pw": permute_wz,
             "f": first_layer, "sq": square, "s": second_layer, "ev": evacuate, "x": scatter, "o": store,
         }
-        for step in [["c2",0],["c1",1,"c"],["c1",1,"d"],["g","xw",0,2],["g","xs",0,2],["c1",0,"a"],["g","zs0",0,2],["q1",1],["g","zs1",0,2],["c1",0,"b"],["q1",0],["pw",0],["g","zw1",0,2],["f",0,1],["g","zw0",0,1],["ps"],["sq",0,1],["g","zw0",1,2],["f",0,0],["c2",1],["q2",0],["sq",0,0],["pw",1],["f",1,0],["s",0,0],["ev",0,0],["q2",1],["s",0,1],["sq",1,0],["ev",0,1],["f",1,1],["sq",1,1],["s",1,0],["x",0,0],["x",0,1],["ev",1,0],["o",0],["s",1,1],["x",1,0],["ev",1,1],["x",1,1],["o",1]]:
+        for step in [["g","xw",0,2],["c1",0,"a"],["c1",1,"c"],["c1",1,"d"],["c1",0,"b"],["g","xs",0,2],["q1",0],["g","zs1",0,2],["g","zs0",0,2],["f",0,0],["ps"],["q1",1],["g","zw0",0,1],["g","zw1",0,2],["pw",0],["pw",1],["sq",0,0],["c2",1],["f",0,1],["c2",0],["q2",1],["q2",0],["sq",0,1],["f",1,0],["s",0,1],["s",0,0],["g","zw0",1,2],["ev",0,1],["sq",1,0],["ev",0,0],["x",0,0],["f",1,1],["x",0,1],["sq",1,1],["o",0],["s",1,0],["s",1,1],["ev",1,0],["x",1,0],["ev",1,1],["x",1,1],["o",1]]:
             if step[0] == "c1":
                 cast_w1(step[1], ["a", "b", "c", "d"].index(step[2]) % 2)
             else:

@@ -17,7 +17,7 @@ FP4X4 = mybir.dt.float4_e2m1fn_x4
 ACT = mybir.ActivationFunctionType
 ALU = mybir.AluOpType
 FUSED = True
-HALF = [[1,1]]
+HALF = []
 C1G = []
 
 
@@ -45,7 +45,7 @@ def tile_moe_mmo_relu2_kernel(
         xs = kt("xs", [P, T], U8)
         zw = [kt("zw%d" % s, [P, Q], I32) for s in range(2)]
         zs = kt("zs", [P, 2, Q], U8)
-        wzw_raw = kt("wzw_raw", [P, 4, 256], I32)
+        wzw_raw = [kt("wzw_raw%d" % e, [P, 2, 256], I32) for e in range(E)]
         wzs_raw = kt("wzs_raw", [P, 4, H], U8)
         w1_raw = [kt("w1_raw%d" % e, [P, 4, H], F32) for e in range(E)]
         w1_s = [kt("w1_s%d" % e, [P, H], U8) for e in range(E)]
@@ -81,8 +81,9 @@ def tile_moe_mmo_relu2_kernel(
                 nc.sync.dma_start(
                     out=wzs_raw[rows].bitcast(I32), in_=wz_scales.rearrange("e s (g r) n -> r g (e s) n", r=4)[q].bitcast(I32)
                 )
-            elif name == "wz":
-                nc.sync.dma_start(out=wzw_raw[:], in_=wz_words.rearrange("e s p n -> p (e s) n").bitcast(I32))
+            elif name[:2] == "wz":
+                e = int(name[2])
+                nc.sync.dma_start(out=wzw_raw[e][:], in_=wz_words[e].rearrange("s p n -> p s n").bitcast(I32))
             elif name[:2] == "w1":
                 e = ["A", "B"].index(name[2])
                 nc.sync.dma_start(out=w1_raw[e][:], in_=w1[e].rearrange("(p j) c -> p j c", j=4))
@@ -93,7 +94,7 @@ def tile_moe_mmo_relu2_kernel(
                 m = int(name[1])
                 nc.sync.dma_start(out=gates[m][:], in_=(gate1, gate2)[m])
 
-        for name in ["w1A","xs0","xs1","xs3","xs2","xw","offs","w1B","zs2","zs1","offs2","zs3","zs0","zw1","ws2","ws3","ws1","ws0","zw0","w212","w211","w203","wz","w201","w213","w200","w210","w202","g1","g0"]:
+        for name in ["w1A","xs0","xs1","xs2","xs3","offs","w1B","offs2","xw","zs0","zs1","zs2","zs3","zw0","ws0","ws1","ws2","ws3","wz0","zw1","w200","w201","w202","w203","w210","w211","w212","w213","wz1","g0","g1"]:
             load(name)
 
         def cast_w1(e, c):
@@ -150,7 +151,7 @@ def tile_moe_mmo_relu2_kernel(
             tl["wzw", e] = vt("wzw%d" % e, [P, 2, 2 * H], U8)
             nc.vector.tensor_copy(
                 out=tl["wzw", e][:].bitcast(I32).rearrange("p s (t b w) -> p s t b w", t=4, w=4),
-                in_=wzw_raw[:, 2 * e : 2 * e + 2].rearrange("p s (b t w) -> p s t b w", t=4, w=4),
+                in_=wzw_raw[e][:].rearrange("p s (b t w) -> p s t b w", t=4, w=4),
             )
 
         def first_layer(m, e):
@@ -234,7 +235,7 @@ def tile_moe_mmo_relu2_kernel(
             "g": gather, "q1": quant_w1, "c2": cast_w2, "q2": quant_w2, "ps": permute_wz_scales, "pw": permute_wz,
             "f": first_layer, "sq": square, "s": second_layer, "ev": evacuate, "x": scatter, "o": store,
         }
-        for step in [["g","xw",0,2],["c1",0,"a"],["c1",1,"c"],["c1",1,"d"],["c1",0,"b"],["g","xs",0,2],["q1",0],["g","zs1",0,2],["g","zs0",0,2],["f",0,0],["ps"],["q1",1],["g","zw0",0,1],["g","zw1",0,2],["pw",0],["pw",1],["sq",0,0],["c2",1],["f",0,1],["c2",0],["q2",1],["q2",0],["sq",0,1],["f",1,0],["s",0,1],["s",0,0],["g","zw0",1,2],["ev",0,1],["sq",1,0],["ev",0,0],["x",0,0],["f",1,1],["x",0,1],["sq",1,1],["o",0],["s",1,0],["s",1,1],["ev",1,0],["x",1,0],["ev",1,1],["x",1,1],["o",1]]:
+        for step in [["g","xs",0,2],["c1",0,"a"],["c1",0,"b"],["c1",1,"c"],["c1",1,"d"],["q1",0],["g","xw",0,2],["f",0,0],["g","zs0",0,2],["g","zs1",0,2],["q1",1],["sq",0,0],["f",0,1],["pw",0],["g","zw0",0,1],["ps"],["g","zw1",0,1],["sq",0,1],["f",1,0],["g","zw0",1,2],["c2",0],["g","zw1",1,2],["q2",0],["c2",1],["s",0,0],["ev",0,0],["q2",1],["s",0,1],["pw",1],["x",0,0],["sq",1,0],["ev",0,1],["f",1,1],["s",1,0],["x",0,1],["o",0],["sq",1,1],["ev",1,0],["s",1,1],["x",1,0],["ev",1,1],["x",1,1],["o",1]]:
             if step[0] == "c1":
                 cast_w1(step[1], ["a", "b", "c", "d"].index(step[2]) % 2)
             else:

from contextlib import ExitStack

import concourse.mybir as mybir

K, L, T, Q, E, C, H, N = 512, 1024, 1024, 1024, 2, 256, 512, 128
P = 128
FLOPS = 2 * E * C * (K * H + L * H + 2 * H * N)

F32 = mybir.dt.float32
BF16 = mybir.dt.bfloat16
I32 = mybir.dt.int32
U32 = mybir.dt.uint32
U16 = mybir.dt.uint16
U8 = mybir.dt.uint8
FP8X4 = mybir.dt.float8_e4m3fn_x4
FP4X4 = mybir.dt.float4_e2m1fn_x4
ACT = mybir.ActivationFunctionType
ALU = mybir.AluOpType
FUSED = True
HALF = []
C1G = []


def tile_moe_mmo_relu2_kernel(
    tc, x_words, x_scales, z_words, z_scales, w1, wz_words, wz_scales, w2, gate1, gate2, offs, offs2, out
):
    nc = tc.nc
    with ExitStack() as ctx:
        keep = ctx.enter_context(tc.tile_pool(name="keep", bufs=1))
        vout = ctx.enter_context(tc.tile_pool(name="vout", bufs=24))
        sout = ctx.enter_context(tc.tile_pool(name="sout", bufs=16))
        psum = ctx.enter_context(tc.psum_pool(name="psum", bufs=8))

        def vt(name, shape, dt):
            return vout.tile(shape, dt, name=name, tag="v", align_bytes=64)

        def sct(name, shape, dt):
            return sout.tile(shape, dt, name=name, tag="s", align_bytes=64)

        def kt(name, shape, dt):
            return keep.tile(shape, dt, name=name, align_bytes=64)

        lists = [kt("liscttext", [P, 32], U16), kt("lisctpatch", [P, 32], U16)]
        xw = kt("xw", [P, T], I32)
        xs = kt("xs", [P, T], U8)
        zw = [kt("zw%d" % s, [P, Q], I32) for s in range(2)]
        zs = kt("zs", [P, 2, Q], U8)
        wzw_raw = [kt("wzw_raw%d" % e, [P, 2, 256], I32) for e in range(E)]
        wzs_raw = kt("wzs_raw", [P, 4, H], U8)
        w1_raw = [kt("w1_raw%d" % e, [P, 4, H], F32) for e in range(E)]
        w1_s = [kt("w1_s%d" % e, [P, H], U8) for e in range(E)]
        w2_raw = kt("w2_raw", [P, E, 4, N], F32)
        gates = [kt("gate%d" % m, [P, E * C], F32) for m in range(2)]
        outs = [kt("out%d" % m, [P, T], F32) for m in range(2)]

        w2_s = [kt("w2_s%d" % e, [P, N], U8) for e in range(E)]
        tl = {}
        nc.vector.memset(xs[:].bitcast(I32), 0)
        nc.vector.memset(zs[:].bitcast(I32), 0)
        nc.vector.memset(wzs_raw[:].bitcast(I32), 0)
        nc.vector.memset(outs[0][:], 0.0)
        nc.vector.memset(outs[1][:], 0.0)

        def load(name):
            q = int(name[2]) if name[:2] in ("xs", "zs", "ws") else 0
            rows = slice(q, P, 32)
            if name == "offs":
                nc.sync.dma_start(lists[0][:], offs)
            elif name == "offs2":
                nc.sync.dma_start(lists[1][:], offs2)
            elif name == "xw":
                nc.sync.dma_start(out=xw[:], in_=x_words[0].rearrange("p t d -> p (t d)").bitcast(I32))
            elif name[:2] == "zw":
                s = int(name[2])
                nc.sync.dma_start(out=zw[s][:], in_=z_words[s].rearrange("p t d -> p (t d)").bitcast(I32))
            elif name[:2] == "xs":
                nc.sync.dma_start(out=xs[rows, :].bitcast(I32), in_=x_scales[0].rearrange("(g r) n -> r g n", r=4)[q].bitcast(I32))
            elif name[:2] == "zs":
                nc.sync.dma_start(out=zs[rows].bitcast(I32), in_=z_scales.rearrange("s (g r) n -> r g s n", r=4)[q].bitcast(I32))
            elif name[:2] == "ws":
                nc.sync.dma_start(
                    out=wzs_raw[rows].bitcast(I32), in_=wz_scales.rearrange("e s (g r) n -> r g (e s) n", r=4)[q].bitcast(I32)
                )
            elif name[:2] == "wz":
                e = int(name[2])
                nc.sync.dma_start(out=wzw_raw[e][:], in_=wz_words[e].rearrange("s p n -> p s n").bitcast(I32))
            elif name[:2] == "w1":
                e = ["A", "B"].index(name[2])
                nc.sync.dma_start(out=w1_raw[e][:], in_=w1[e].rearrange("(p j) c -> p j c", j=4))
            elif name[:2] == "w2":
                e, j = int(name[2]), int(name[3])
                nc.sync.dma_start(out=w2_raw[:, e, j, :], in_=w2[e].rearrange("(b j u) n -> j b u n", j=4, u=8)[j])
            else:
                m = int(name[1])
                nc.sync.dma_start(out=gates[m][:], in_=(gate1, gate2)[m])

        for name in ["w1A","xs0","xs1","xs2","xs3","offs","w1B","offs2","xw","zs0","zs1","zs2","zs3","zw0","ws0","ws1","ws2","ws3","wz0","zw1","w200","w201","w202","w203","w210","w211","w212","w213","wz1","g0","g1"]:
            load(name)

        def cast_w1(e, c):
            if c == 0:
                tl["w1_bf", e] = (kt if [e, c] in C1G else sct)("w1_bf%d" % e, [P, H, 4], BF16)
            for t in (2 * c, 2 * c + 1):
                nc.scalar.copy(
                    out=tl["w1_bf", e][:].rearrange("p (t b h l) j -> p t b h j l", t=4, h=2, l=4)[:, t],
                    in_=w1_raw[e][:].rearrange("p j (b t h l) -> p t b h j l", t=4, h=2, l=4)[:, t],
                )

        def quant_w1(e):
            tl["w1_c", e] = vt("w1_c%d" % e, [P, H], U32)
            nc.vector.quantize_mx(
                out=tl["w1_c", e][:].bitcast(FP8X4), scales=w1_s[e][:], in_=tl["w1_bf", e][:].rearrange("p c j -> p (c j)")
            )

        def cast_w2(e):
            tl["w2_bf", e] = vt("w2_bf%d" % e, [P, N, 4], BF16)
            nc.vector.tensor_copy(
                out=tl["w2_bf", e][:].rearrange("p (a l) j -> p a j l", l=4), in_=w2_raw[:, e].rearrange("p j (a l) -> p a j l", l=4)
            )

        def quant_w2(e):
            tl["w2_c", e] = vt("w2_c%d" % e, [P, N], U32)
            nc.vector.quantize_mx(
                out=tl["w2_c", e][:].bitcast(FP8X4), scales=w2_s[e][:], in_=tl["w2_bf", e][:].rearrange("p n j -> p (n j)")
            )

        windows = {
            "xw": (U32, xw[:].bitcast(U32), 0),
            "xs": (U8, xs[:], 0),
            "zw0": (U32, zw[0][:].bitcast(U32), 1),
            "zw1": (U32, zw[1][:].bitcast(U32), 1),
            "zs0": (U8, zs[:, 0, :], 1),
            "zs1": (U8, zs[:, 1, :], 1),
        }

        def gather(what, e0, e1):
            dt, window, m = windows[what]
            dst = vt("g_%s%d" % (what, e0), [P, (e1 - e0) * C], dt)
            nc.vector.tensor_copy(dst[:], window.indirect(lists[m][:, 16 * e0 : 16 * e1]))
            for e in range(e0, e1):
                tl[what, e] = dst[:, (e - e0) * C : (e - e0 + 1) * C]

        def permute_wz_scales():
            tl["wzs"] = vt("wzs", [P, 4, H], U8)
            nc.vector.tensor_copy(
                out=tl["wzs"][:].bitcast(I32).rearrange("p g (t b w) -> p g t b w", t=4, w=2),
                in_=wzs_raw[:].bitcast(I32).rearrange("p g (b t w) -> p g t b w", t=4, w=2),
            )

        def permute_wz(e):
            tl["wzw", e] = vt("wzw%d" % e, [P, 2, 2 * H], U8)
            nc.vector.tensor_copy(
                out=tl["wzw", e][:].bitcast(I32).rearrange("p s (t b w) -> p s t b w", t=4, w=4),
                in_=wzw_raw[e][:].rearrange("p s (b t w) -> p s t b w", t=4, w=4),
            )

        def first_layer(m, e):
            pos = sct("pos%d%d" % (m, e), [P, 2, 128, 4], F32)
            for half in range(2):
                cols = slice(half * 128, half * 128 + 128)
                bank = psum.tile([P, 4, 128], F32, name="bank", tag="bank")
                for t in range(4):
                    if m == 0:
                        nc.tensor.matmul_mx(
                            out=bank[:, t, :],
                            lhsT=tl["w1_c", e][:, 128 * t : 128 * t + 128].bitcast(FP8X4),
                            lhsT_scale=w1_s[e][:, 128 * t : 128 * t + 128],
                            rhs=tl["xw", e][:, cols].bitcast(FP8X4),
                            rhs_scale=tl["xs", e][:, cols],
                            start=True,
                            stop=True,
                        )
                    else:
                        for s in range(2):
                            nc.tensor.matmul_mx(
                                out=bank[:, t, :],
                                lhsT=tl["wzw", e][:, s, 256 * t : 256 * t + 256].bitcast(FP4X4),
                                lhsT_scale=tl["wzs"][:, 2 * e + s, 128 * t : 128 * t + 128],
                                rhs=tl["zw%d" % s, e][:, cols].bitcast(FP8X4),
                                rhs_scale=tl["zs%d" % s, e][:, cols],
                                start=(s == 0),
                                stop=(s == 1),
                            )
                nc.scalar.activation(pos[:, half], bank[:].rearrange("p t n -> p n t"), ACT.Relu)
            tl["pos", m, e] = pos

        def pieces(m, e):
            return ((0, 128), (128, 256)) if [m, e] in HALF else ((0, 256),)

        def square(m, e):
            act = sct("act%d%d" % (m, e), [P, C * 4], BF16)
            flat = tl["pos", m, e][:].rearrange("p h n t -> p (h n t)")
            for lo, hi in pieces(m, e):
                nc.scalar.activation(act[:, 4 * lo : 4 * hi], flat[:, 4 * lo : 4 * hi], ACT.Square)
            tl["act", m, e] = act

        def second_layer(m, e):
            hc = vt("hc%d%d" % (m, e), [P, C], U32)
            hs = kt("hs%d%d" % (m, e), [P, C], U8)
            for lo, hi in pieces(m, e):
                nc.vector.quantize_mx(out=hc[:, lo:hi].bitcast(FP8X4), scales=hs[:, lo:hi], in_=tl["act", m, e][:, 4 * lo : 4 * hi])
                acc = psum.tile([P, hi - lo], F32, name="acc", tag="bank")
                nc.tensor.matmul_mx(
                    out=acc[:],
                    lhsT=tl["w2_c", e][:].bitcast(FP8X4),
                    lhsT_scale=w2_s[e][:],
                    rhs=hc[:, lo:hi].bitcast(FP8X4),
                    rhs_scale=hs[:, lo:hi],
                    start=True,
                    stop=True,
                )
                tl["acc", m, e, lo] = acc

        def evacuate(m, e):
            ev = sct("ev%d%d" % (m, e), [P, C], F32)
            for lo, hi in pieces(m, e):
                if FUSED:
                    nc.scalar.copy(ev[:, lo:hi], tl["acc", m, e, lo][:])
                else:
                    nc.vector.tensor_tensor(ev[:, lo:hi], tl["acc", m, e, lo][:], gates[m][:, e * C + lo : e * C + hi], ALU.mult)
            tl["ev", m, e] = ev

        def scatter(m, e):
            for lo, hi in pieces(m, e):
                window = outs[m][:].indirect(lists[m][:, (e * C + lo) // 16 : (e * C + hi) // 16])
                if FUSED:
                    nc.vector.tensor_tensor(window, tl["ev", m, e][:, lo:hi], gates[m][:, e * C + lo : e * C + hi], ALU.mult)
                else:
                    nc.vector.tensor_copy(window, tl["ev", m, e][:, lo:hi])

        def store(m):
            nc.sync.dma_start(out=out[:, m * T : (m + 1) * T], in_=outs[m][:])

        table = {
            "g": gather, "q1": quant_w1, "c2": cast_w2, "q2": quant_w2, "ps": permute_wz_scales, "pw": permute_wz,
            "f": first_layer, "sq": square, "s": second_layer, "ev": evacuate, "x": scatter, "o": store,
        }
        for step in [["g","xs",0,2],["c1",0,"a"],["c1",0,"b"],["c1",1,"c"],["c1",1,"d"],["q1",0],["g","xw",0,2],["f",0,0],["g","zs0",0,2],["g","zs1",0,2],["q1",1],["sq",0,0],["f",0,1],["pw",0],["g","zw0",0,1],["ps"],["g","zw1",0,1],["sq",0,1],["f",1,0],["g","zw0",1,2],["c2",0],["g","zw1",1,2],["q2",0],["c2",1],["s",0,0],["ev",0,0],["q2",1],["s",0,1],["pw",1],["x",0,0],["sq",1,0],["ev",0,1],["f",1,1],["s",1,0],["x",0,1],["o",0],["sq",1,1],["ev",1,0],["s",1,1],["x",1,0],["ev",1,1],["x",1,1],["o",1]]:
            if step[0] == "c1":
                cast_w1(step[1], ["a", "b", "c", "d"].index(step[2]) % 2)
            else:
                table[step[0]](*step[1:])
